import numpy as np
CORES = [7,391,135,263,15,399,143,271]
N = 8
R, W, T = 4096, 64, 256
CAPP = 64
def entries(a): return a.T.reshape(-1)
def pack(v, P): return np.ascontiguousarray(np.asarray(v, np.int32).reshape(-1, P).T)
def lists(rng, how):
    Q = rng.permutation(N * R)[:N * T]
    if how == "hotrank": Q = R * int(rng.integers(N)) + rng.permutation(R)[:N * T]
    if how == "own": Q = np.concatenate([R * r + rng.permutation(R)[:T] for r in range(N)])
    if how == "sorted": Q = np.sort(Q)
    if how == "edge":
        ends = np.concatenate([R * np.arange(N), R * np.arange(N) + R - 1]); rest = np.setdiff1d(rng.permutation(N * R), ends, assume_unique=True)
        Q = rng.permutation(np.concatenate([ends, rng.permutation(rest)[:N * T - 2 * N]]))
    if how in ("uniform", "full", "sorted", "edge"):
        O = np.stack([rng.permutation(np.repeat(rng.permutation(N)[:T // CAPP], CAPP)) if how == "full" else rng.permutation(np.repeat(np.arange(N), CAPP))[:T] for r in range(N)]).reshape(-1); Q = np.zeros(N * T, np.int64)
        for d in range(N):
            m = np.nonzero(O == d)[0]; w = rng.permutation(R)[:len(m)]
            if how == "edge" and len(m) >= 2: w[:2] = [0, R - 1]; w[2:] = 1 + rng.permutation(R - 2)[:len(m) - 2]
            Q[m] = R * d + w
        if how == "sorted": Q = np.sort(Q.reshape(N, T), axis=1).reshape(-1)
    return {"pos": np.stack([pack(q, 128) for q in Q.reshape(N, T)])}
def setup_inputs(rng):
    return dict({"tab": rng.standard_normal((N, R, W), dtype=np.float32), "new": rng.standard_normal((N, T, W), dtype=np.float32)}, **lists(rng, "uniform"))
def setup_inputs_edge(rng):
    d = setup_inputs(rng); d.update(lists(rng, "edge"))
    for k in ("tab", "new"): d[k] = (d[k].astype(np.float32) * 1048576.0).astype(d[k].dtype)
    return d
def setup_inputs_full(rng):
    d = setup_inputs(rng); d.update(lists(rng, "full"))
    for k in ("tab", "new"): d[k] = (d[k].astype(np.float32) * (1 / 1024.0)).astype(d[k].dtype)
    return d
def setup_inputs_sorted(rng):
    d = setup_inputs(rng); d.update(lists(rng, "sorted"))
    return d
def check_inputs(x):
    bad = []
    if x["pos"].min() < 0 or x["pos"].max() >= N * R: bad.append("pos out of range")
    if len(np.unique(x["pos"])) != x["pos"].size: bad.append("a place is named twice")
    if max(int(np.bincount(entries(a) // R, minlength=N).max()) for a in x["pos"]) > CAPP: bad.append("more than CAPP entries of a list point into one rank's part")
    return bad
def reference(tab, new, pos):
    A = np.concatenate(list(tab), axis=0)
    for r in range(N): A[entries(pos[r])] = new[r]
    return {"y": np.stack([A[R * r:R * r + R] for r in range(N)])}

@@ -1,0 +1,206 @@
+from concourse.bass import IndirectOffsetOnAxis
+from concourse.mybir import AluOpType, ActivationFunctionType
+
+NB = 33
+RW = 2 * NB
+FW = 65
+
+SCRATCH = {
+    "posT": ("sbuf", [128, 2], "int32"),
+    "own_i": ("sbuf", [128, 2], "int32"),
+    "loc_i": ("sbuf", [128, 2], "int32"),
+    "own_f": ("sbuf", [128, 2], "float32"),
+    "iota8": ("sbuf", [128, 8], "float32"),
+    "iota64": ("sbuf", [128, 64], "float32"),
+    "ones_b": ("sbuf", [128, 128], "bfloat16"),
+    "tri_b": ("sbuf", [128, 128], "bfloat16"),
+    "hot8": ("sbuf", [128, 24], "bfloat16"),
+    "hot8f": ("sbuf", [128, 16], "float32"),
+    "newx": ("sbuf", [128, 2 * RW], "float32"),
+    "onehot": ("sbuf", [128, 1024], "float32"),
+    "blk": ("sbuf", [128, 7 * NB], "float32"),
+    "landM": ("sbuf", [128, NB], "float32"),
+    "landW": ("sbuf", [128, 4 * NB], "float32"),
+    "landN": ("sbuf", [128, 2 * NB], "float32"),
+    "landF": ("sbuf", [128, 2 * NB], "float32"),
+    "rows": ("sbuf", [128, 4 * FW], "float32"),
+    "idxT": ("sbuf", [128, 4], "int32"),
+    "cnt": ("psum", [128, 512], "float32"),
+    "ps0": ("psum", [128, 512], "float32"),
+    "ps1": ("psum", [128, 512], "float32"),
+    "ps2": ("psum", [128, 512], "float32"),
+    "ps3": ("psum", [128, 512], "float32"),
+}
+SEMAPHORES = ["lpos", "lnew", "pad", "ones", "iot", "tri", "sa", "sb", "sc", "sd", "sdf", "sx", "scnt",
+              "p0", "p1", "p2", "p3", "m0", "m1", "m2", "m3", "e0", "e1", "e2", "e3",
+              "as0", "as1", "as2", "as3", "f0", "f1", "f2", "f3",
+              "aM", "aW", "aN", "aF", "sent", "cpg", "cp", "scat"]
+
+
+def _ring(T, topo):
+    by_host = {}
+    for c in T.cores:
+        by_host.setdefault(topo.host(c), []).append(c)
+    for h in by_host:
+        by_host[h].sort(key=topo.chip)
+    hs = sorted(by_host)
+
+    def nbrs(h):
+        return [k for k in hs if k != h and topo.may_write(by_host[h][0], by_host[k][0])]
+    ring = [hs[0]]
+    ring.append([k for k in nbrs(hs[0]) if topo.rack(k) == topo.rack(hs[0])][0])
+    while len(ring) < len(hs):
+        ring.append([k for k in nbrs(ring[-1]) if k not in ring][0])
+    return ring, by_host
+
+
+def _bits(m):
+    return bin(m).count("1")
+
+
+def rank_program(g, core, T, topo):
+    rank = T.rank_of(core)
+    if rank is None:
+        return
+    v, s, pe, sy, S = g.vector, g.scalar, g.tensor, g.sync, T.sem
+    Copy = ActivationFunctionType.Copy
+    ring, by_host = _ring(T, topo)
+    i = ring.index(topo.host(core))
+    side = by_host[ring[i]].index(core)
+    mate = by_host[ring[i]][1 - side]
+    nxt, prv, dia = (by_host[ring[(i + k) % 4]] for k in (1, 3, 2))
+    order = [core, mate, nxt[0], nxt[1], dia[0], dia[1], prv[0], prv[1]]
+    col = {mate: 0, prv[0]: 5 * NB, prv[1]: 6 * NB}
+    for k in (0, 1):
+        col[nxt[k]] = (1 + 2 * k + side) * NB
+        col[dia[k]] = (1 + 2 * k + 1 - side) * NB
+
+    sy.dma_start(T.posT[:], T.pos[:]).then_inc(S.lpos, 16)
+    v.memset(T.newx[:], 0.0).then_inc(S.pad, 1)
+    v.memset(T.ones_b[:], 1.0).then_inc(S.ones, 1)
+    v.memset(T.hot8[:, 0:8], 0.0).then_inc(S.sd, 1)
+    s.wait_ge(S.pad, 1)
+    for c in (0, 1):
+        s.dma_start(T.newx[:, c * RW + 1:c * RW + 65], T.new[c * 128:(c + 1) * 128, :]).then_inc(S.lnew, 16)
+    g.iota(T.iota8[:], [[1, 8]], 0, 0, allow_small_or_imprecise_dtypes=True).then_inc(S.iot, 1)
+    g.iota(T.iota64[:], [[1, 64]], 0, 0, allow_small_or_imprecise_dtypes=True).then_inc(S.iot, 1)
+    g.wait_ge(S.ones, 1)
+    g.affine_select(T.tri_b[:], T.ones_b[:], [[1, 128]], AluOpType.is_gt, 0.0, 0, -1).then_inc(S.tri, 1)
+    g.dma_start(T.y[0:1024, :], T.tab[0:1024, :]).then_inc(S.cpg, 16)
+    sy.dma_start(T.y[1024:2560, :], T.tab[1024:2560, :]).then_inc(S.cp, 16)
+    s.dma_start(T.y[2560:4096, :], T.tab[2560:4096, :]).then_inc(S.cp, 16)
+
+    v.wait_ge(S.lpos, 16)
+    v.tensor_scalar(T.own_i[:], T.posT[:], 12, None, AluOpType.logical_shift_right).then_inc(S.sa, 1)
+    v.tensor_scalar(T.loc_i[:], T.posT[:], 4095, None, AluOpType.bitwise_and).then_inc(S.sb, 1)
+    v.wait_ge(S.sa, 1)
+    v.tensor_copy(T.own_f[:], T.own_i[:]).then_inc(S.sc, 1)
+    v.wait_ge(S.sc, 1)
+    v.wait_ge(S.iot, 2)
+    for c in (0, 1):
+        v.tensor_scalar(T.hot8[:, 8 + 8 * c:16 + 8 * c], T.iota8[:], T.own_f[:, c:c + 1], None,
+                        AluOpType.is_equal).then_inc(S.sd, 1)
+    for c in (0, 1):
+        v.tensor_scalar(T.hot8f[:, 8 * c:8 + 8 * c], T.iota8[:], T.own_f[:, c:c + 1], None,
+                        AluOpType.is_equal).then_inc(S.sdf, 1)
+    v.wait_ge(S.sb, 1)
+    v.wait_ge(S.lnew, 32)
+    for c in (0, 1):
+        v.tensor_scalar(T.newx[:, c * RW:c * RW + 1], T.loc_i[:, c:c + 1], 1, None, AluOpType.add).then_inc(S.sx, 1)
+    pe.wait_ge(S.sd, 3)
+    pe.wait_ge(S.tri, 1)
+    pe.wait_ge(S.ones, 1)
+    pe.matmul(T.cnt[:, 0:16], T.tri_b[:], T.hot8[:, 8:24], start=True, stop=False)
+    pe.matmul(T.cnt[:, 0:16], T.ones_b[:], T.hot8[:, 0:16], start=False, stop=True).then_inc(S.scnt, 1)
+    v.wait_ge(S.scnt, 1)
+    v.wait_ge(S.sdf, 2)
+    for rel, dst in enumerate(order):
+        d = T.rank_of(dst)
+        for c in (0, 1):
+            v.tensor_scalar(T.onehot[:, c * 512 + rel * 64:c * 512 + rel * 64 + 64], T.iota64[:],
+                            T.cnt[:, 8 * c + d:8 * c + d + 1], T.hot8f[:, 8 * c + d:8 * c + d + 1],
+                            AluOpType.is_equal, AluOpType.mult).then_inc(S["p%d" % (rel // 2)], 1)
+    pe.wait_ge(S.sx, 2)
+    for t in range(4):
+        pe.wait_ge(S["p%d" % t], 4)
+        ps = T["ps%d" % t]
+        pe.matmul(ps[:, 0:RW], T.onehot[:, t * 128:t * 128 + 128], T.newx[:, 0:RW], start=True, stop=False)
+        pe.matmul(ps[:, 0:RW], T.onehot[:, 512 + t * 128:512 + t * 128 + 128], T.newx[:, RW:2 * RW],
+                  start=False, stop=True).then_inc(S["m%d" % t], 1)
+    for t in range(4):
+        s.wait_ge(S["m%d" % t], 1)
+        ps = T["ps%d" % t]
+        for h in (1, 0) if t == 0 else (0, 1):
+            dst = order[2 * t + h]
+            if dst == core:
+                s.activation(T.rows[0:64, 0:FW], ps[0:64, 0:FW], Copy).then_inc(S.as0, 1)
+                continue
+            a = col[dst]
+            s.activation(T.blk[0:64, a:a + NB], ps[64 * h:64 * h + 64, 0:NB], Copy).then_inc(S["e%d" % t], 1)
+            s.activation(T.blk[64:128, a:a + NB], ps[64 * h:64 * h + 64, NB:RW], Copy).then_inc(S["e%d" % t], 1)
+
+    sent = [0]
+
+    def send(dst, out_ap, in_ap, sem):
+        rid, pid = topo.addr(dst, core)
+        m = topo.mask(core, dst)
+        g.remote_dma(out_ap, in_ap, sem, S.sent, pid, rid, m)
+        sent[0] += _bits(m)
+
+    g.wait_ge(S.e0, 2)
+    send(mate, T.landM[:], T.blk[:, 0:NB], S.aM)
+    g.wait_ge(S.e1, 4)
+    g.wait_ge(S.e2, 4)
+    for k in (side, 1 - side):
+        send(nxt[k], T.landW[:, 2 * NB * side:2 * NB * side + 2 * NB], T.blk[:, (1 + 2 * k) * NB:(3 + 2 * k) * NB], S.aW)
+    g.wait_ge(S.e3, 4)
+    for k in (side, 1 - side):
+        send(prv[k], T.landN[:, NB * side:NB * side + NB], T.blk[:, (5 + k) * NB:(6 + k) * NB], S.aN)
+
+    nM = _bits(topo.mask(mate, core))
+    nW = sum(_bits(topo.mask(c, core)) for c in prv)
+    nN = sum(_bits(topo.mask(c, core)) for c in nxt)
+    nF = _bits(topo.mask(prv[side], core))
+    arrive = [(S.aM, nM), (S.aW, nW), (S.aN, nN), (S.aF, nF)]
+    bufs = [(None, (T.landM, 0)), ((T.landW, 0), (T.landW, 3 * NB)), ((T.landN, 0), (T.landN, NB)),
+            ((T.landF, 0), (T.landF, NB))]
+    for t in range(4):
+        sem, n = arrive[t]
+        f0 = t * FW
+        asm = S["as%d" % t]
+        v.wait_ge(sem, n)
+        s.wait_ge(sem, n)
+        top, bot = bufs[t]
+        if top is None:
+            b, a = bot
+            v.tensor_copy(T.rows[64:128, f0:f0 + NB], b[0:64, a:a + NB]).then_inc(asm, 1)
+            s.activation(T.rows[64:128, f0 + NB:f0 + FW], b[64:128, a:a + 32], Copy).then_inc(asm, 1)
+            need = 3
+        else:
+            b, a = top
+            v.tensor_copy(T.rows[0:64, f0:f0 + NB], b[0:64, a:a + NB]).then_inc(asm, 1)
+            v.tensor_copy(T.rows[0:64, f0 + NB:f0 + FW], b[64:128, a:a + 32]).then_inc(asm, 1)
+            b, a = bot
+            s.activation(T.rows[64:128, f0:f0 + NB], b[0:64, a:a + NB], Copy).then_inc(asm, 1)
+            s.activation(T.rows[64:128, f0 + NB:f0 + FW], b[64:128, a:a + 32], Copy).then_inc(asm, 1)
+            need = 4
+        v.wait_ge(asm, need)
+        v.tensor_scalar(T.idxT[:, t:t + 1], T.rows[:, f0:f0 + 1], -1, None, AluOpType.add).then_inc(S["f%d" % t], 1)
+
+    def scatter(t):
+        g.wait_ge(S["f%d" % t], 1)
+        g.wait_ge(S["as%d" % t], 3 if t == 0 else 4)
+        g.indirect_dma_start(T.y[:], IndirectOffsetOnAxis(ap=T.idxT[:, t:t + 1], axis=0),
+                             T.rows[:, t * FW + 1:t * FW + FW], None, bounds_check=4095,
+                             oob_is_err=False).then_inc(S.scat, 16)
+
+    g.wait_ge(S.cpg, 16)
+    g.wait_ge(S.cp, 32)
+    scatter(0)
+    g.wait_ge(S.aW, nW)
+    send(nxt[side], T.landF[:], T.landW[:, NB:3 * NB], S.aF)
+    scatter(1)
+    scatter(2)
+    scatter(3)
+    g.wait_ge(S.scat, 64)
+    g.wait_ge(S.sent, sent[0])

@@ -1,9 +1,11 @@
-from concourse.bass import IndirectOffsetOnAxis
+from concourse.bass import DstId, RemoteDMATransfer, IndirectOffsetOnAxis
 from concourse.mybir import AluOpType, ActivationFunctionType
 
 NB = 33
 RW = 2 * NB
 FW = 65
+CS = 68
+PART = 4096
 
 SCRATCH = {
     "posT": ("sbuf", [128, 2], "int32"),
@@ -16,16 +18,25 @@ SCRATCH = {
     "tri_b": ("sbuf", [128, 128], "bfloat16"),
     "hot8": ("sbuf", [128, 24], "bfloat16"),
     "hot8f": ("sbuf", [128, 16], "float32"),
-    "newx": ("sbuf", [128, 2 * RW], "float32"),
+    "newx": ("sbuf", [128, 2 * CS + 4], "float32"),
     "onehot": ("sbuf", [128, 1024], "float32"),
     "blk": ("sbuf", [128, 7 * NB], "float32"),
+    "posM": ("sbuf", [128, 2], "int32"),
+    "ownm_i": ("sbuf", [128, 2], "int32"),
+    "eqm_b": ("sbuf", [128, 4], "bfloat16"),
+    "eqm_f": ("sbuf", [128, 2], "float32"),
+    "locm_f": ("sbuf", [128, 2], "float32"),
+    "ohm": ("sbuf", [128, 256], "float32"),
     "landM": ("sbuf", [128, NB], "float32"),
-    "landW": ("sbuf", [128, 4 * NB], "float32"),
+    "landW": ("sbuf", [128, 2 * NB], "float32"),
     "landN": ("sbuf", [128, 2 * NB], "float32"),
     "landF": ("sbuf", [128, 2 * NB], "float32"),
+    "landR": ("sbuf", [128, 2 * NB], "float32"),
     "rows": ("sbuf", [128, 4 * FW], "float32"),
     "idxT": ("sbuf", [128, 4], "int32"),
     "cnt": ("psum", [128, 512], "float32"),
+    "cntm": ("psum", [128, 512], "float32"),
+    "psI": ("psum", [128, 512], "float32"),
     "ps0": ("psum", [128, 512], "float32"),
     "ps1": ("psum", [128, 512], "float32"),
     "ps2": ("psum", [128, 512], "float32"),
@@ -33,8 +44,9 @@ SCRATCH = {
 }
 SEMAPHORES = ["lpos", "lnew", "pad", "ones", "iot", "tri", "sa", "sb", "sc", "sd", "sdf", "sx", "scnt",
               "p0", "p1", "p2", "p3", "m0", "m1", "m2", "m3", "e0", "e1", "e2", "e3",
-              "as0", "as1", "as2", "as3", "f0", "f1", "f2", "f3",
-              "aM", "aW", "aN", "aF", "sent", "cpg", "cp", "scat"]
+              "ow", "as0", "as1", "as2", "as3", "f0", "f1", "f2", "f3",
+              "la", "lb", "lc", "ld", "le", "lf", "lg",
+              "aL", "aM", "aW", "aN", "aF", "aR", "sent", "cpg", "cp", "scat"]
 
 
 def _ring(T, topo):
@@ -54,90 +66,69 @@ def _ring(T, topo):
     return ring, by_host
 
 
+def _relays(T, topo, ring, by_host):
+    relay = {}
+    for i, h in enumerate(ring):
+        for k, x in enumerate(by_host[h]):
+            tgt = by_host[ring[(i + 1) % len(ring)]][k]
+            relay[x] = [c for c in range(max(0, x - 16), x + 16)
+                        if c not in T.cores and topo.host(c) == topo.host(x) and topo.chip(c) == topo.chip(x)
+                        and topo.die(c) == topo.die(x) and topo.may_write(c, tgt)][0]
+    return relay
+
+
 def _bits(m):
     return bin(m).count("1")
 
 
+def _halves(m):
+    b = [1 << k for k in range(m.bit_length()) if (m >> k) & 1]
+    return sum(b[:len(b) // 2]), sum(b[len(b) // 2:])
+
+
 def rank_program(g, core, T, topo):
+    S = T.sem
+    ring, by_host = _ring(T, topo)
+    relay = _relays(T, topo, ring, by_host)
     rank = T.rank_of(core)
     if rank is None:
+        for x, q in relay.items():
+            if q != core:
+                continue
+            ix = ring.index(topo.host(x))
+            k = by_host[ring[ix]].index(x)
+            tgt = by_host[ring[(ix + 1) % 4]][k]
+            g.wait_ge(S.aR, sum(_bits(_halves(topo.mask(c, core))[k]) for c in by_host[ring[(ix + 3) % 4]]))
+            rid, pid = topo.addr(tgt, core)
+            m = topo.mask(core, tgt)
+            g.remote_dma(T.landF[:], T.landR[:], S.aF, S.sent, pid, rid, m)
+            g.wait_ge(S.sent, _bits(m))
         return
-    v, s, pe, sy, S = g.vector, g.scalar, g.tensor, g.sync, T.sem
+    v, s, pe, sy = g.vector, g.scalar, g.tensor, g.sync
     Copy = ActivationFunctionType.Copy
-    ring, by_host = _ring(T, topo)
     i = ring.index(topo.host(core))
     side = by_host[ring[i]].index(core)
     mate = by_host[ring[i]][1 - side]
     nxt, prv, dia = (by_host[ring[(i + k) % 4]] for k in (1, 3, 2))
     order = [core, mate, nxt[0], nxt[1], dia[0], dia[1], prv[0], prv[1]]
-    col = {mate: 0, prv[0]: 5 * NB, prv[1]: 6 * NB}
-    for k in (0, 1):
-        col[nxt[k]] = (1 + 2 * k + side) * NB
-        col[dia[k]] = (1 + 2 * k + 1 - side) * NB
+    col = {dst: (n - 1) * NB for n, dst in enumerate(order) if n}
 
     sy.dma_start(T.posT[:], T.pos[:]).then_inc(S.lpos, 16)
-    v.memset(T.newx[:], 0.0).then_inc(S.pad, 1)
+    sy.dma_start(T.newx[:, 4:CS], T.new[0:128, :]).then_inc(S.lnew, 16)
+    s.dma_start(T.newx[:, CS + 4:2 * CS], T.new[128:256, :]).then_inc(S.lnew, 16)
+    sy.dma_start(T.y[512:2304, :], T.tab[512:2304, :]).then_inc(S.cp, 16)
+    s.dma_start(T.y[2304:4096, :], T.tab[2304:4096, :]).then_inc(S.cp, 16)
     v.memset(T.ones_b[:], 1.0).then_inc(S.ones, 1)
     v.memset(T.hot8[:, 0:8], 0.0).then_inc(S.sd, 1)
-    s.wait_ge(S.pad, 1)
+    v.memset(T.newx[:, CS:CS + 3], 0.0).then_inc(S.pad, 1)
+    v.memset(T.newx[:, 2 * CS:2 * CS + 4], 0.0).then_inc(S.pad, 1)
+    v.memset(T.eqm_b[:, 0:1], 0.0).then_inc(S.lc, 1)
     for c in (0, 1):
-        s.dma_start(T.newx[:, c * RW + 1:c * RW + 65], T.new[c * 128:(c + 1) * 128, :]).then_inc(S.lnew, 16)
+        v.memset(T.ohm[:, c * 128:c * 128 + 64], 0.0).then_inc(S.lf, 1)
     g.iota(T.iota8[:], [[1, 8]], 0, 0, allow_small_or_imprecise_dtypes=True).then_inc(S.iot, 1)
     g.iota(T.iota64[:], [[1, 64]], 0, 0, allow_small_or_imprecise_dtypes=True).then_inc(S.iot, 1)
     g.wait_ge(S.ones, 1)
     g.affine_select(T.tri_b[:], T.ones_b[:], [[1, 128]], AluOpType.is_gt, 0.0, 0, -1).then_inc(S.tri, 1)
-    g.dma_start(T.y[0:1024, :], T.tab[0:1024, :]).then_inc(S.cpg, 16)
-    sy.dma_start(T.y[1024:2560, :], T.tab[1024:2560, :]).then_inc(S.cp, 16)
-    s.dma_start(T.y[2560:4096, :], T.tab[2560:4096, :]).then_inc(S.cp, 16)
-
-    v.wait_ge(S.lpos, 16)
-    v.tensor_scalar(T.own_i[:], T.posT[:], 12, None, AluOpType.logical_shift_right).then_inc(S.sa, 1)
-    v.tensor_scalar(T.loc_i[:], T.posT[:], 4095, None, AluOpType.bitwise_and).then_inc(S.sb, 1)
-    v.wait_ge(S.sa, 1)
-    v.tensor_copy(T.own_f[:], T.own_i[:]).then_inc(S.sc, 1)
-    v.wait_ge(S.sc, 1)
-    v.wait_ge(S.iot, 2)
-    for c in (0, 1):
-        v.tensor_scalar(T.hot8[:, 8 + 8 * c:16 + 8 * c], T.iota8[:], T.own_f[:, c:c + 1], None,
-                        AluOpType.is_equal).then_inc(S.sd, 1)
-    for c in (0, 1):
-        v.tensor_scalar(T.hot8f[:, 8 * c:8 + 8 * c], T.iota8[:], T.own_f[:, c:c + 1], None,
-                        AluOpType.is_equal).then_inc(S.sdf, 1)
-    v.wait_ge(S.sb, 1)
-    v.wait_ge(S.lnew, 32)
-    for c in (0, 1):
-        v.tensor_scalar(T.newx[:, c * RW:c * RW + 1], T.loc_i[:, c:c + 1], 1, None, AluOpType.add).then_inc(S.sx, 1)
-    pe.wait_ge(S.sd, 3)
-    pe.wait_ge(S.tri, 1)
-    pe.wait_ge(S.ones, 1)
-    pe.matmul(T.cnt[:, 0:16], T.tri_b[:], T.hot8[:, 8:24], start=True, stop=False)
-    pe.matmul(T.cnt[:, 0:16], T.ones_b[:], T.hot8[:, 0:16], start=False, stop=True).then_inc(S.scnt, 1)
-    v.wait_ge(S.scnt, 1)
-    v.wait_ge(S.sdf, 2)
-    for rel, dst in enumerate(order):
-        d = T.rank_of(dst)
-        for c in (0, 1):
-            v.tensor_scalar(T.onehot[:, c * 512 + rel * 64:c * 512 + rel * 64 + 64], T.iota64[:],
-                            T.cnt[:, 8 * c + d:8 * c + d + 1], T.hot8f[:, 8 * c + d:8 * c + d + 1],
-                            AluOpType.is_equal, AluOpType.mult).then_inc(S["p%d" % (rel // 2)], 1)
-    pe.wait_ge(S.sx, 2)
-    for t in range(4):
-        pe.wait_ge(S["p%d" % t], 4)
-        ps = T["ps%d" % t]
-        pe.matmul(ps[:, 0:RW], T.onehot[:, t * 128:t * 128 + 128], T.newx[:, 0:RW], start=True, stop=False)
-        pe.matmul(ps[:, 0:RW], T.onehot[:, 512 + t * 128:512 + t * 128 + 128], T.newx[:, RW:2 * RW],
-                  start=False, stop=True).then_inc(S["m%d" % t], 1)
-    for t in range(4):
-        s.wait_ge(S["m%d" % t], 1)
-        ps = T["ps%d" % t]
-        for h in (1, 0) if t == 0 else (0, 1):
-            dst = order[2 * t + h]
-            if dst == core:
-                s.activation(T.rows[0:64, 0:FW], ps[0:64, 0:FW], Copy).then_inc(S.as0, 1)
-                continue
-            a = col[dst]
-            s.activation(T.blk[0:64, a:a + NB], ps[64 * h:64 * h + 64, 0:NB], Copy).then_inc(S["e%d" % t], 1)
-            s.activation(T.blk[64:128, a:a + NB], ps[64 * h:64 * h + 64, NB:RW], Copy).then_inc(S["e%d" % t], 1)
 
     sent = [0]
 
@@ -147,60 +138,136 @@ def rank_program(g, core, T, topo):
         g.remote_dma(out_ap, in_ap, sem, S.sent, pid, rid, m)
         sent[0] += _bits(m)
 
+    def pair(dsts, blocks, out_ap, sem):
+        tr = []
+        for k in (0, 1):
+            rid, pid = topo.addr(dsts[k], core)
+            m = _halves(topo.mask(core, dsts[k]))[k]
+            a = col[blocks[k]]
+            tr.append(RemoteDMATransfer(dst_ids=[DstId(rid=rid, pnc=pid)], dma_engine_mask=m, remote_sem=sem,
+                                        src=T.blk[:, a:a + NB], dst=out_ap))
+            sent[0] += _bits(m)
+        g.remote_dma_fused(tr, local_sem=S.sent)
+
+    g.wait_ge(S.lpos, 16)
+    send(mate, T.posM[:], T.posT[:], S.aL)
+    g.dma_start(T.y[0:512, :], T.tab[0:512, :]).then_inc(S.cpg, 16)
+
+    v.wait_ge(S.lpos, 16)
+    v.tensor_scalar(T.own_i[:], T.posT[:], 12, None, AluOpType.logical_shift_right).then_inc(S.sa, 1)
+    v.tensor_scalar(T.loc_i[:], T.posT[:], PART - 1, None, AluOpType.bitwise_and).then_inc(S.sb, 1)
+    v.wait_ge(S.sa, 1)
+    v.tensor_copy(T.own_f[:], T.own_i[:]).then_inc(S.sc, 1)
+    v.wait_ge(S.sc, 1)
+    v.wait_ge(S.iot, 2)
+    for c in (0, 1):
+        v.tensor_scalar(T.hot8[:, 8 + 8 * c:16 + 8 * c], T.iota8[:], T.own_f[:, c:c + 1], None,
+                        AluOpType.is_equal).then_inc(S.sd, 1)
+    v.wait_ge(S.sb, 1)
+    for c in (0, 1):
+        v.tensor_scalar(T.newx[:, c * CS + 3:c * CS + 4], T.loc_i[:, c:c + 1], 1, None,
+                        AluOpType.add).then_inc(S.sx, 1)
+    s.wait_ge(S.sd, 3)
+    s.activation(T.hot8f[:], T.hot8[:, 8:24], Copy).then_inc(S.sdf, 1)
+    pe.wait_ge(S.sd, 3)
+    pe.wait_ge(S.tri, 1)
+    pe.wait_ge(S.ones, 1)
+    pe.matmul(T.cnt[:, 0:16], T.tri_b[:], T.hot8[:, 8:24], start=True, stop=False)
+    pe.matmul(T.cnt[:, 0:16], T.ones_b[:], T.hot8[:, 0:16], start=False, stop=True).then_inc(S.scnt, 1)
+    v.wait_ge(S.scnt, 1)
+    v.wait_ge(S.sdf, 1)
+    for rel, dst in enumerate(order):
+        d = T.rank_of(dst)
+        for c in (0, 1):
+            v.tensor_scalar(T.onehot[:, c * 512 + rel * 64:c * 512 + rel * 64 + 64], T.iota64[:],
+                            T.cnt[:, 8 * c + d:8 * c + d + 1], T.hot8f[:, 8 * c + d:8 * c + d + 1],
+                            AluOpType.is_equal, AluOpType.mult).then_inc(S["p%d" % (rel // 2)], 1)
+    pe.wait_ge(S.sx, 2)
+    pe.wait_ge(S.lnew, 32)
+    pe.wait_ge(S.pad, 2)
+    for t in range(4):
+        pe.wait_ge(S["p%d" % t], 4)
+        ps = T["ps%d" % t]
+        pe.matmul(ps[:, 0:RW], T.onehot[:, t * 128:t * 128 + 128], T.newx[:, 3:3 + RW], start=True, stop=False)
+        pe.matmul(ps[:, 0:RW], T.onehot[:, 512 + t * 128:512 + t * 128 + 128], T.newx[:, CS + 3:CS + 3 + RW],
+                  start=False, stop=True).then_inc(S["m%d" % t], 1)
+    for t in range(4):
+        s.wait_ge(S["m%d" % t], 1)
+        ps = T["ps%d" % t]
+        for h in (1, 0) if t == 0 else (0, 1):
+            dst = order[2 * t + h]
+            if dst == core:
+                s.activation(T.rows[0:64, 0:FW], ps[0:64, 0:FW], Copy).then_inc(S.ow, 1)
+                continue
+            a = col[dst]
+            s.activation(T.blk[0:64, a:a + NB], ps[64 * h:64 * h + 64, 0:NB], Copy).then_inc(S["e%d" % t], 1)
+            s.activation(T.blk[64:128, a:a + NB], ps[64 * h:64 * h + 64, NB:RW], Copy).then_inc(S["e%d" % t], 1)
+
+    mine = slice(NB * side, NB * side + NB)
     g.wait_ge(S.e0, 2)
-    send(mate, T.landM[:], T.blk[:, 0:NB], S.aM)
+    send(mate, T.landM[:], T.blk[:, col[mate]:col[mate] + NB], S.aM)
     g.wait_ge(S.e1, 4)
+    pair(nxt, nxt, T.landW[:, mine], S.aW)
     g.wait_ge(S.e2, 4)
-    for k in (side, 1 - side):
-        send(nxt[k], T.landW[:, 2 * NB * side:2 * NB * side + 2 * NB], T.blk[:, (1 + 2 * k) * NB:(3 + 2 * k) * NB], S.aW)
+    pair([relay[nxt[0]], relay[nxt[1]]], dia, T.landR[:, mine], S.aR)
     g.wait_ge(S.e3, 4)
-    for k in (side, 1 - side):
-        send(prv[k], T.landN[:, NB * side:NB * side + NB], T.blk[:, (5 + k) * NB:(6 + k) * NB], S.aN)
+    pair(prv, prv, T.landN[:, mine], S.aN)
+
+    v.wait_ge(S.ow, 1)
+    v.tensor_scalar(T.idxT[0:64, 0:1], T.rows[0:64, 0:1], -1, None, AluOpType.add).then_inc(S.f0, 1)
+    v.wait_ge(S.aL, _bits(topo.mask(mate, core)))
+    v.tensor_scalar(T.ownm_i[:], T.posM[:], 12, None, AluOpType.logical_shift_right).then_inc(S.la, 1)
+    v.tensor_scalar(T.locm_f[:], T.posM[:], 1 - PART * rank, None, AluOpType.add).then_inc(S.lb, 1)
+    v.wait_ge(S.la, 1)
+    v.tensor_scalar(T.eqm_b[:, 1:3], T.ownm_i[:], rank, None, AluOpType.is_equal).then_inc(S.lc, 1)
+    v.tensor_scalar(T.eqm_f[:], T.ownm_i[:], rank, None, AluOpType.is_equal).then_inc(S.ld, 1)
+    pe.wait_ge(S.lc, 2)
+    pe.matmul(T.cntm[:, 0:2], T.tri_b[:], T.eqm_b[:, 1:3], start=True, stop=False)
+    pe.matmul(T.cntm[:, 0:2], T.ones_b[:], T.eqm_b[:, 0:2], start=False, stop=True).then_inc(S.le, 1)
+    v.wait_ge(S.le, 1)
+    v.wait_ge(S.ld, 1)
+    for c in (0, 1):
+        v.tensor_scalar(T.ohm[:, c * 128 + 64:c * 128 + 128], T.iota64[:], T.cntm[:, c:c + 1], T.eqm_f[:, c:c + 1],
+                        AluOpType.is_equal, AluOpType.mult).then_inc(S.lf, 1)
+    pe.wait_ge(S.lf, 4)
+    pe.wait_ge(S.lb, 1)
+    pe.matmul(T.psI[:, 0:1], T.ohm[:, 0:128], T.locm_f[:, 0:1], start=True, stop=False)
+    pe.matmul(T.psI[:, 0:1], T.ohm[:, 128:256], T.locm_f[:, 1:2], start=False, stop=True).then_inc(S.lg, 1)
+    v.wait_ge(S.lg, 1)
+    v.tensor_scalar(T.idxT[64:128, 0:1], T.psI[64:128, 0:1], -1, None, AluOpType.add).then_inc(S.f0, 1)
 
     nM = _bits(topo.mask(mate, core))
-    nW = sum(_bits(topo.mask(c, core)) for c in prv)
-    nN = sum(_bits(topo.mask(c, core)) for c in nxt)
-    nF = _bits(topo.mask(prv[side], core))
-    arrive = [(S.aM, nM), (S.aW, nW), (S.aN, nN), (S.aF, nF)]
-    bufs = [(None, (T.landM, 0)), ((T.landW, 0), (T.landW, 3 * NB)), ((T.landN, 0), (T.landN, NB)),
-            ((T.landF, 0), (T.landF, NB))]
-    for t in range(4):
-        sem, n = arrive[t]
+    nW = sum(_bits(_halves(topo.mask(c, core))[side]) for c in prv)
+    nN = sum(_bits(_halves(topo.mask(c, core))[side]) for c in nxt)
+    nF = _bits(topo.mask(relay[prv[side]], core))
+    s.wait_ge(S.aM, nM)
+    s.activation(T.rows[64:128, 0:NB], T.landM[0:64, 0:NB], Copy).then_inc(S.as0, 1)
+    s.activation(T.rows[64:128, NB:FW], T.landM[64:128, 0:32], Copy).then_inc(S.as0, 1)
+    arrive = [None, (S.aW, nW, T.landW), (S.aN, nN, T.landN), (S.aF, nF, T.landF)]
+    for t in (1, 2, 3):
+        sem, n, b = arrive[t]
         f0 = t * FW
         asm = S["as%d" % t]
         v.wait_ge(sem, n)
         s.wait_ge(sem, n)
-        top, bot = bufs[t]
-        if top is None:
-            b, a = bot
-            v.tensor_copy(T.rows[64:128, f0:f0 + NB], b[0:64, a:a + NB]).then_inc(asm, 1)
-            s.activation(T.rows[64:128, f0 + NB:f0 + FW], b[64:128, a:a + 32], Copy).then_inc(asm, 1)
-            need = 3
-        else:
-            b, a = top
-            v.tensor_copy(T.rows[0:64, f0:f0 + NB], b[0:64, a:a + NB]).then_inc(asm, 1)
-            v.tensor_copy(T.rows[0:64, f0 + NB:f0 + FW], b[64:128, a:a + 32]).then_inc(asm, 1)
-            b, a = bot
-            s.activation(T.rows[64:128, f0:f0 + NB], b[0:64, a:a + NB], Copy).then_inc(asm, 1)
-            s.activation(T.rows[64:128, f0 + NB:f0 + FW], b[64:128, a:a + 32], Copy).then_inc(asm, 1)
-            need = 4
-        v.wait_ge(asm, need)
+        v.tensor_copy(T.rows[0:64, f0:f0 + NB], b[0:64, 0:NB]).then_inc(asm, 1)
+        v.tensor_copy(T.rows[0:64, f0 + NB:f0 + FW], b[64:128, 0:32]).then_inc(asm, 1)
+        s.activation(T.rows[64:128, f0:f0 + NB], b[0:64, NB:2 * NB], Copy).then_inc(asm, 1)
+        s.activation(T.rows[64:128, f0 + NB:f0 + FW], b[64:128, NB:NB + 32], Copy).then_inc(asm, 1)
+        v.wait_ge(asm, 4)
         v.tensor_scalar(T.idxT[:, t:t + 1], T.rows[:, f0:f0 + 1], -1, None, AluOpType.add).then_inc(S["f%d" % t], 1)
 
     def scatter(t):
-        g.wait_ge(S["f%d" % t], 1)
-        g.wait_ge(S["as%d" % t], 3 if t == 0 else 4)
+        g.wait_ge(S["f%d" % t], 2 if t == 0 else 1)
+        g.wait_ge(S["as%d" % t], 2 if t == 0 else 4)
         g.indirect_dma_start(T.y[:], IndirectOffsetOnAxis(ap=T.idxT[:, t:t + 1], axis=0),
-                             T.rows[:, t * FW + 1:t * FW + FW], None, bounds_check=4095,
+                             T.rows[:, t * FW + 1:t * FW + FW], None, bounds_check=PART - 1,
                              oob_is_err=False).then_inc(S.scat, 16)
 
     g.wait_ge(S.cpg, 16)
     g.wait_ge(S.cp, 32)
-    scatter(0)
-    g.wait_ge(S.aW, nW)
-    send(nxt[side], T.landF[:], T.landW[:, NB:3 * NB], S.aF)
-    scatter(1)
-    scatter(2)
-    scatter(3)
+    g.wait_ge(S.ow, 1)
+    for t in range(4):
+        scatter(t)
     g.wait_ge(S.scat, 64)
     g.wait_ge(S.sent, sent[0])

from concourse.bass import DstId, RemoteDMATransfer, IndirectOffsetOnAxis
from concourse.mybir import AluOpType, ActivationFunctionType

NB = 33
RW = 2 * NB
FW = 65
CS = 68
PART = 4096

SCRATCH = {
    "posT": ("sbuf", [128, 2], "int32"),
    "own_i": ("sbuf", [128, 2], "int32"),
    "loc_i": ("sbuf", [128, 2], "int32"),
    "own_f": ("sbuf", [128, 2], "float32"),
    "iota8": ("sbuf", [128, 8], "float32"),
    "iota64": ("sbuf", [128, 64], "float32"),
    "ones_b": ("sbuf", [128, 128], "bfloat16"),
    "tri_b": ("sbuf", [128, 128], "bfloat16"),
    "hot8": ("sbuf", [128, 24], "bfloat16"),
    "hot8f": ("sbuf", [128, 16], "float32"),
    "newx": ("sbuf", [128, 2 * CS + 4], "float32"),
    "onehot": ("sbuf", [128, 1024], "float32"),
    "blk": ("sbuf", [128, 7 * NB], "float32"),
    "posM": ("sbuf", [128, 2], "int32"),
    "ownm_i": ("sbuf", [128, 2], "int32"),
    "eqm_b": ("sbuf", [128, 4], "bfloat16"),
    "eqm_f": ("sbuf", [128, 2], "float32"),
    "locm_f": ("sbuf", [128, 2], "float32"),
    "ohm": ("sbuf", [128, 256], "float32"),
    "landM": ("sbuf", [128, NB], "float32"),
    "landW": ("sbuf", [128, 2 * NB], "float32"),
    "landN": ("sbuf", [128, 2 * NB], "float32"),
    "landF": ("sbuf", [128, 2 * NB], "float32"),
    "landR": ("sbuf", [128, 2 * NB], "float32"),
    "rows": ("sbuf", [128, 4 * FW], "float32"),
    "idxT": ("sbuf", [128, 4], "int32"),
    "cnt": ("psum", [128, 512], "float32"),
    "cntm": ("psum", [128, 512], "float32"),
    "psI": ("psum", [128, 512], "float32"),
    "ps0": ("psum", [128, 512], "float32"),
    "ps1": ("psum", [128, 512], "float32"),
    "ps2": ("psum", [128, 512], "float32"),
    "ps3": ("psum", [128, 512], "float32"),
}
SEMAPHORES = ["lpos", "lnew", "pad", "ones", "iot", "tri", "sa", "sb", "sc", "sd", "sdf", "sx", "scnt",
              "p0", "p1", "p2", "p3", "m0", "m1", "m2", "m3", "e0", "e1", "e2", "e3",
              "ow", "as0", "as1", "as2", "as3", "f0", "f1", "f2", "f3",
              "la", "lb", "lc", "ld", "le", "lf", "lg",
              "aL", "aM", "aW", "aN", "aF", "aR", "sent", "cpg", "cp", "scat"]


def _ring(T, topo):
    by_host = {}
    for c in T.cores:
        by_host.setdefault(topo.host(c), []).append(c)
    for h in by_host:
        by_host[h].sort(key=topo.chip)
    hs = sorted(by_host)

    def nbrs(h):
        return [k for k in hs if k != h and topo.may_write(by_host[h][0], by_host[k][0])]
    ring = [hs[0]]
    ring.append([k for k in nbrs(hs[0]) if topo.rack(k) == topo.rack(hs[0])][0])
    while len(ring) < len(hs):
        ring.append([k for k in nbrs(ring[-1]) if k not in ring][0])
    return ring, by_host


def _relays(T, topo, ring, by_host):
    relay = {}
    for i, h in enumerate(ring):
        for k, x in enumerate(by_host[h]):
            tgt = by_host[ring[(i + 1) % len(ring)]][k]
            relay[x] = [c for c in range(max(0, x - 16), x + 16)
                        if c not in T.cores and topo.host(c) == topo.host(x) and topo.chip(c) == topo.chip(x)
                        and topo.die(c) == topo.die(x) and topo.may_write(c, tgt)][0]
    return relay


def _bits(m):
    return bin(m).count("1")


def _halves(m):
    b = [1 << k for k in range(m.bit_length()) if (m >> k) & 1]
    return sum(b[:len(b) // 2]), sum(b[len(b) // 2:])


def rank_program(g, core, T, topo):
    S = T.sem
    ring, by_host = _ring(T, topo)
    relay = _relays(T, topo, ring, by_host)
    rank = T.rank_of(core)
    if rank is None:
        for x, q in relay.items():
            if q != core:
                continue
            ix = ring.index(topo.host(x))
            k = by_host[ring[ix]].index(x)
            tgt = by_host[ring[(ix + 1) % 4]][k]
            g.wait_ge(S.aR, sum(_bits(_halves(topo.mask(c, core))[k]) for c in by_host[ring[(ix + 3) % 4]]))
            rid, pid = topo.addr(tgt, core)
            m = topo.mask(core, tgt)
            g.remote_dma(T.landF[:], T.landR[:], S.aF, S.sent, pid, rid, m)
            g.wait_ge(S.sent, _bits(m))
        return
    v, s, pe, sy = g.vector, g.scalar, g.tensor, g.sync
    Copy = ActivationFunctionType.Copy
    i = ring.index(topo.host(core))
    side = by_host[ring[i]].index(core)
    mate = by_host[ring[i]][1 - side]
    nxt, prv, dia = (by_host[ring[(i + k) % 4]] for k in (1, 3, 2))
    order = [core, mate, nxt[0], nxt[1], dia[0], dia[1], prv[0], prv[1]]
    col = {dst: (n - 1) * NB for n, dst in enumerate(order) if n}

    sy.dma_start(T.posT[:], T.pos[:]).then_inc(S.lpos, 16)
    sy.dma_start(T.newx[:, 4:CS], T.new[0:128, :]).then_inc(S.lnew, 16)
    s.dma_start(T.newx[:, CS + 4:2 * CS], T.new[128:256, :]).then_inc(S.lnew, 16)
    sy.dma_start(T.y[512:2304, :], T.tab[512:2304, :]).then_inc(S.cp, 16)
    s.dma_start(T.y[2304:4096, :], T.tab[2304:4096, :]).then_inc(S.cp, 16)
    v.memset(T.ones_b[:], 1.0).then_inc(S.ones, 1)
    v.memset(T.hot8[:, 0:8], 0.0).then_inc(S.sd, 1)
    v.memset(T.newx[:, CS:CS + 3], 0.0).then_inc(S.pad, 1)
    v.memset(T.newx[:, 2 * CS:2 * CS + 4], 0.0).then_inc(S.pad, 1)
    v.memset(T.eqm_b[:, 0:1], 0.0).then_inc(S.lc, 1)
    for c in (0, 1):
        v.memset(T.ohm[:, c * 128:c * 128 + 64], 0.0).then_inc(S.lf, 1)
    g.iota(T.iota8[:], [[1, 8]], 0, 0, allow_small_or_imprecise_dtypes=True).then_inc(S.iot, 1)
    g.iota(T.iota64[:], [[1, 64]], 0, 0, allow_small_or_imprecise_dtypes=True).then_inc(S.iot, 1)
    g.wait_ge(S.ones, 1)
    g.affine_select(T.tri_b[:], T.ones_b[:], [[1, 128]], AluOpType.is_gt, 0.0, 0, -1).then_inc(S.tri, 1)

    sent = [0]

    def send(dst, out_ap, in_ap, sem):
        rid, pid = topo.addr(dst, core)
        m = topo.mask(core, dst)
        g.remote_dma(out_ap, in_ap, sem, S.sent, pid, rid, m)
        sent[0] += _bits(m)

    def pair(dsts, blocks, out_ap, sem):
        tr = []
        for k in (0, 1):
            rid, pid = topo.addr(dsts[k], core)
            m = _halves(topo.mask(core, dsts[k]))[k]
            a = col[blocks[k]]
            tr.append(RemoteDMATransfer(dst_ids=[DstId(rid=rid, pnc=pid)], dma_engine_mask=m, remote_sem=sem,
                                        src=T.blk[:, a:a + NB], dst=out_ap))
            sent[0] += _bits(m)
        g.remote_dma_fused(tr, local_sem=S.sent)

    g.wait_ge(S.lpos, 16)
    send(mate, T.posM[:], T.posT[:], S.aL)
    g.dma_start(T.y[0:512, :], T.tab[0:512, :]).then_inc(S.cpg, 16)

    v.wait_ge(S.lpos, 16)
    v.tensor_scalar(T.own_i[:], T.posT[:], 12, None, AluOpType.logical_shift_right).then_inc(S.sa, 1)
    v.tensor_scalar(T.loc_i[:], T.posT[:], PART - 1, None, AluOpType.bitwise_and).then_inc(S.sb, 1)
    v.wait_ge(S.sa, 1)
    v.tensor_copy(T.own_f[:], T.own_i[:]).then_inc(S.sc, 1)
    v.wait_ge(S.sc, 1)
    v.wait_ge(S.iot, 2)
    for c in (0, 1):
        v.tensor_scalar(T.hot8[:, 8 + 8 * c:16 + 8 * c], T.iota8[:], T.own_f[:, c:c + 1], None,
                        AluOpType.is_equal).then_inc(S.sd, 1)
    v.wait_ge(S.sb, 1)
    for c in (0, 1):
        v.tensor_scalar(T.newx[:, c * CS + 3:c * CS + 4], T.loc_i[:, c:c + 1], 1, None,
                        AluOpType.add).then_inc(S.sx, 1)
    s.wait_ge(S.sd, 3)
    s.activation(T.hot8f[:], T.hot8[:, 8:24], Copy).then_inc(S.sdf, 1)
    pe.wait_ge(S.sd, 3)
    pe.wait_ge(S.tri, 1)
    pe.wait_ge(S.ones, 1)
    pe.matmul(T.cnt[:, 0:16], T.tri_b[:], T.hot8[:, 8:24], start=True, stop=False)
    pe.matmul(T.cnt[:, 0:16], T.ones_b[:], T.hot8[:, 0:16], start=False, stop=True).then_inc(S.scnt, 1)
    v.wait_ge(S.scnt, 1)
    v.wait_ge(S.sdf, 1)
    for rel, dst in enumerate(order):
        d = T.rank_of(dst)
        for c in (0, 1):
            v.tensor_scalar(T.onehot[:, c * 512 + rel * 64:c * 512 + rel * 64 + 64], T.iota64[:],
                            T.cnt[:, 8 * c + d:8 * c + d + 1], T.hot8f[:, 8 * c + d:8 * c + d + 1],
                            AluOpType.is_equal, AluOpType.mult).then_inc(S["p%d" % (rel // 2)], 1)
    pe.wait_ge(S.sx, 2)
    pe.wait_ge(S.lnew, 32)
    pe.wait_ge(S.pad, 2)
    for t in range(4):
        pe.wait_ge(S["p%d" % t], 4)
        ps = T["ps%d" % t]
        pe.matmul(ps[:, 0:RW], T.onehot[:, t * 128:t * 128 + 128], T.newx[:, 3:3 + RW], start=True, stop=False)
        pe.matmul(ps[:, 0:RW], T.onehot[:, 512 + t * 128:512 + t * 128 + 128], T.newx[:, CS + 3:CS + 3 + RW],
                  start=False, stop=True).then_inc(S["m%d" % t], 1)
    for t in range(4):
        s.wait_ge(S["m%d" % t], 1)
        ps = T["ps%d" % t]
        for h in (1, 0) if t == 0 else (0, 1):
            dst = order[2 * t + h]
            if dst == core:
                s.activation(T.rows[0:64, 0:FW], ps[0:64, 0:FW], Copy).then_inc(S.ow, 1)
                continue
            a = col[dst]
            s.activation(T.blk[0:64, a:a + NB], ps[64 * h:64 * h + 64, 0:NB], Copy).then_inc(S["e%d" % t], 1)
            s.activation(T.blk[64:128, a:a + NB], ps[64 * h:64 * h + 64, NB:RW], Copy).then_inc(S["e%d" % t], 1)

    mine = slice(NB * side, NB * side + NB)
    g.wait_ge(S.e0, 2)
    send(mate, T.landM[:], T.blk[:, col[mate]:col[mate] + NB], S.aM)
    g.wait_ge(S.e1, 4)
    pair(nxt, nxt, T.landW[:, mine], S.aW)
    g.wait_ge(S.e2, 4)
    pair([relay[nxt[0]], relay[nxt[1]]], dia, T.landR[:, mine], S.aR)
    g.wait_ge(S.e3, 4)
    pair(prv, prv, T.landN[:, mine], S.aN)

    v.wait_ge(S.ow, 1)
    v.tensor_scalar(T.idxT[0:64, 0:1], T.rows[0:64, 0:1], -1, None, AluOpType.add).then_inc(S.f0, 1)
    v.wait_ge(S.aL, _bits(topo.mask(mate, core)))
    v.tensor_scalar(T.ownm_i[:], T.posM[:], 12, None, AluOpType.logical_shift_right).then_inc(S.la, 1)
    v.tensor_scalar(T.locm_f[:], T.posM[:], 1 - PART * rank, None, AluOpType.add).then_inc(S.lb, 1)
    v.wait_ge(S.la, 1)
    v.tensor_scalar(T.eqm_b[:, 1:3], T.ownm_i[:], rank, None, AluOpType.is_equal).then_inc(S.lc, 1)
    v.tensor_scalar(T.eqm_f[:], T.ownm_i[:], rank, None, AluOpType.is_equal).then_inc(S.ld, 1)
    pe.wait_ge(S.lc, 2)
    pe.matmul(T.cntm[:, 0:2], T.tri_b[:], T.eqm_b[:, 1:3], start=True, stop=False)
    pe.matmul(T.cntm[:, 0:2], T.ones_b[:], T.eqm_b[:, 0:2], start=False, stop=True).then_inc(S.le, 1)
    v.wait_ge(S.le, 1)
    v.wait_ge(S.ld, 1)
    for c in (0, 1):
        v.tensor_scalar(T.ohm[:, c * 128 + 64:c * 128 + 128], T.iota64[:], T.cntm[:, c:c + 1], T.eqm_f[:, c:c + 1],
                        AluOpType.is_equal, AluOpType.mult).then_inc(S.lf, 1)
    pe.wait_ge(S.lf, 4)
    pe.wait_ge(S.lb, 1)
    pe.matmul(T.psI[:, 0:1], T.ohm[:, 0:128], T.locm_f[:, 0:1], start=True, stop=False)
    pe.matmul(T.psI[:, 0:1], T.ohm[:, 128:256], T.locm_f[:, 1:2], start=False, stop=True).then_inc(S.lg, 1)
    v.wait_ge(S.lg, 1)
    v.tensor_scalar(T.idxT[64:128, 0:1], T.psI[64:128, 0:1], -1, None, AluOpType.add).then_inc(S.f0, 1)

    nM = _bits(topo.mask(mate, core))
    nW = sum(_bits(_halves(topo.mask(c, core))[side]) for c in prv)
    nN = sum(_bits(_halves(topo.mask(c, core))[side]) for c in nxt)
    nF = _bits(topo.mask(relay[prv[side]], core))
    s.wait_ge(S.aM, nM)
    s.activation(T.rows[64:128, 0:NB], T.landM[0:64, 0:NB], Copy).then_inc(S.as0, 1)
    s.activation(T.rows[64:128, NB:FW], T.landM[64:128, 0:32], Copy).then_inc(S.as0, 1)
    arrive = [None, (S.aW, nW, T.landW), (S.aN, nN, T.landN), (S.aF, nF, T.landF)]
    for t in (1, 2, 3):
        sem, n, b = arrive[t]
        f0 = t * FW
        asm = S["as%d" % t]
        v.wait_ge(sem, n)
        s.wait_ge(sem, n)
        v.tensor_copy(T.rows[0:64, f0:f0 + NB], b[0:64, 0:NB]).then_inc(asm, 1)
        v.tensor_copy(T.rows[0:64, f0 + NB:f0 + FW], b[64:128, 0:32]).then_inc(asm, 1)
        s.activation(T.rows[64:128, f0:f0 + NB], b[0:64, NB:2 * NB], Copy).then_inc(asm, 1)
        s.activation(T.rows[64:128, f0 + NB:f0 + FW], b[64:128, NB:NB + 32], Copy).then_inc(asm, 1)
        v.wait_ge(asm, 4)
        v.tensor_scalar(T.idxT[:, t:t + 1], T.rows[:, f0:f0 + 1], -1, None, AluOpType.add).then_inc(S["f%d" % t], 1)

    def scatter(t):
        g.wait_ge(S["f%d" % t], 2 if t == 0 else 1)
        g.wait_ge(S["as%d" % t], 2 if t == 0 else 4)
        g.indirect_dma_start(T.y[:], IndirectOffsetOnAxis(ap=T.idxT[:, t:t + 1], axis=0),
                             T.rows[:, t * FW + 1:t * FW + FW], None, bounds_check=PART - 1,
                             oob_is_err=False).then_inc(S.scat, 16)

    g.wait_ge(S.cpg, 16)
    g.wait_ge(S.cp, 32)
    g.wait_ge(S.ow, 1)
    for t in range(4):
        scatter(t)
    g.wait_ge(S.scat, 64)
    g.wait_ge(S.sent, sent[0])
